import numpy as np
import ml_dtypes


def mxq(x, axis, fmt="e4m3"):
    dtype, down = {"e4m3": (ml_dtypes.float8_e4m3fn, 7), "e5m2": (ml_dtypes.float8_e5m2, 14)}[fmt]
    v = np.moveaxis(np.asarray(x, np.float32).astype(ml_dtypes.bfloat16).astype(np.float64), axis, -1)
    blocks = v.reshape(v.shape[:-1] + (-1, 32))
    amax = np.abs(blocks).max(-1, keepdims=True)
    byte = np.maximum(np.where(amax > 0, np.frexp(amax)[1] - 1 + 127, 0) - down, 1)
    scale = np.exp2(byte - 127.0)
    codes = (blocks / scale).astype(np.float32).astype(dtype).astype(np.float64)
    return np.moveaxis((codes * scale).reshape(v.shape), -1, axis)


WIDE = False


def mx_kscale(k):
    if not WIDE:
        return np.ones(k)
    levels = np.array([10, -10, 5, -5, 0])
    if k % 512:
        return np.exp2(np.random.permutation(np.resize(levels, k // 32))).repeat(32)
    a = np.empty((k // 512, 16))
    for p in range(k // 512):
        a[p, :8] = np.random.permutation(np.resize(levels, 8))
        for g in range(8):
            far = levels[np.abs(levels - a[p, g]) >= 10]
            a[p, g + 8] = far[np.random.randint(len(far))]
    return np.exp2(a.ravel()).repeat(32)


def f64(x):
    return np.asarray(x).astype(np.float64)


def striped(idx):
    return np.tile(idx.reshape(-1, 16).T, (8, 1)).astype(np.uint16)


def unstriped(offs):
    return offs[:16].T.reshape(-1).astype(np.int64)


def striped8(idx):
    return np.concatenate([x.reshape(-1, 16).T for x in idx]).astype(np.uint16)


def runs(offs, k):
    lists = np.stack([offs[16 * r : 16 * r + 16].T.reshape(-1) for r in range(8)]).astype(np.int64)
    return lists[np.arange(k) % 512 // 64]


def pack_weight(w):
    k, n = w.shape
    w = f64(np.asarray(w, np.float32).astype(ml_dtypes.bfloat16)).reshape(k // 32, 32, n)
    amax = np.abs(w).max(1)
    byte = np.clip(np.where(amax > 0, np.frexp(amax)[1] - 1 + 127 - 7, 1), 1, 254)
    scaled = (w * np.exp2(127.0 - byte)[:, None, :]).reshape(k, n).astype(np.float32)
    words = np.ascontiguousarray(scaled.reshape(k // 512, 128, 4, n).transpose(0, 1, 3, 2)).astype(ml_dtypes.float8_e4m3fn).view(np.uint8)
    return words, np.ascontiguousarray(byte.astype(np.uint8).reshape(k // 512, 16, n))


def unpack_weight(words, scales):
    g, p, n, _ = words.shape
    vals = np.ascontiguousarray(words).view(ml_dtypes.float8_e4m3fn).astype(np.float64) * np.repeat(np.exp2(scales.astype(np.float64) - 127.0), 8, axis=1)[..., None]
    return vals.transpose(0, 1, 3, 2).reshape(g * 512, n)

def planes(y):
    n, m = y.shape
    v = y.astype(np.float32).astype(ml_dtypes.bfloat16).astype(np.float64).reshape(n // 32, 32, m)
    top = np.abs(v).max(1)
    byte = np.clip(np.where(top > 0, np.frexp(top)[1] - 1 + 127 - 7, 1), 1, 254)
    codes = (v * np.exp2(127.0 - byte)[:, None, :]).reshape(n, m).astype(np.float32).astype(ml_dtypes.float8_e4m3fn).view(np.uint8)
    words = codes.reshape(n // 512, 128, 4, m).transpose(0, 1, 3, 2)
    return np.ascontiguousarray(words), np.ascontiguousarray(byte.astype(np.uint8).reshape(n // 512, 16, m))


K, T, S, N, H = 512, 2048, 512, 512, 512


def setup_inputs():
    n = np.random.standard_normal
    s = mx_kscale(K)[:, None]
    u = mx_kscale(H)
    packed_xT = pack_weight(n((K, T)) * s)
    packed_w3 = pack_weight(n((H, N)) / np.sqrt(H) / u[:, None])
    return {
        "x_words": packed_xT[0],
        "x_scales": packed_xT[1],
        "w1": (n((K, H)) / np.sqrt(K) / s * u).astype(np.float32),
        "w2": (n((H, H)) / np.sqrt(H) / u[:, None] * u).astype(np.float32),
        "w3_words": packed_w3[0],
        "w3_scales": packed_w3[1],
        "res": n((N, S)).astype(np.float32),
        "offs": striped(np.random.permutation(T)[:S]),
        "n1": striped8(np.stack([np.random.permutation(S) for _ in range(8)])),
        "n2": striped8(np.stack([np.random.permutation(S) for _ in range(8)])),
        "n3": striped8(np.stack([np.random.permutation(S) for _ in range(8)])),
        "n4": striped8(np.stack([np.random.permutation(S) for _ in range(8)])),
    }


def reference(x_words, x_scales, w1, w2, w3_words, w3_scales, res, offs, n1, n2, n3, n4):
    xq = unpack_weight(x_words, x_scales)[:, unstriped(offs)]
    y = mxq(f64(w1), 0, "e4m3").T @ xq
    z = y[np.arange(H)[:, None], runs(n1, H)] + 0.75 * (y[np.arange(H)[:, None], runs(n2, H)])
    h = mxq(f64(w2), 0, "e4m3").T @ mxq(z, 0, "e4m3")
    z2 = np.minimum(np.maximum(h, h[np.arange(H)[:, None], runs(n3, H)]), h[np.arange(H)[:, None], runs(n4, H)])
    out_0 = f64(res) + (unpack_weight(w3_words, w3_scales).T @ mxq(z2, 0, "e4m3"))
    return (out_0,) + planes(out_0)

@@ -1,0 +1,229 @@
+from contextlib import ExitStack
+
+import concourse.mybir as mybir
+
+K, T, S, N, H = 512, 2048, 512, 512, 512
+FLOPS = 2 * K * H * S + 2 * H * H * S + 2 * H * N * S
+
+F32 = mybir.dt.float32
+BF16 = mybir.dt.bfloat16
+U32 = mybir.dt.uint32
+I32 = mybir.dt.int32
+U16 = mybir.dt.uint16
+U8 = mybir.dt.uint8
+FP8X4 = mybir.dt.float8_e4m3fn_x4
+ALU = mybir.AluOpType
+
+P = 128
+PACK = 4
+CHUNKS = (256, 128, 128)
+W1_ON_VECTOR = 80
+RING = 3
+
+
+def tile_picked_deepsumminmx_none_po_kernel(tc, x_words, x_scales, w1, w2, w3_words, w3_scales, res, offs, n1, n2, n3, n4, out_0, out_1, out_2):
+    nc = tc.nc
+    with ExitStack() as ctx:
+        lists = ctx.enter_context(tc.tile_pool(name="lists", bufs=1))
+        sb = ctx.enter_context(tc.tile_pool(name="sb", bufs=1))
+        psum = ctx.enter_context(tc.psum_pool(name="psum", bufs=8))
+
+        def sbuf(name, shape, dtype, tag=None):
+            return sb.tile(shape, dtype, name=name, tag=tag or name, align_bytes=64)
+
+        def load_list(name, src):
+            t = lists.tile([P, S // 16], U16, name=name)
+            nc.sync.dma_start(t[:], src)
+            return t
+
+        def load_scale_rows(dst, src):
+            for q in range(4):
+                nc.sync.dma_start(dst[32 * q : 32 * q + 4, :].bitcast(I32), src[0][4 * q : 4 * q + 4, :].bitcast(I32))
+
+        def words_view(dram):
+            return dram[0].rearrange("p n t -> p (n t)").bitcast(I32)
+
+        def entries(lst, c0, n):
+            return lst[:, c0 // 16 : (c0 + n) // 16]
+
+        def copy_on(engine, out, in_):
+            if engine == "vector":
+                nc.vector.tensor_copy(out, in_)
+            else:
+                nc.scalar.copy(out, in_)
+
+        def deal_weight(engine, dst, raw, m0, m1):
+            copy_on(
+                engine,
+                dst[:].rearrange("p (t m j) -> p m t j", t=PACK, j=PACK)[:, m0:m1],
+                raw[:].rearrange("p j (m t) -> p m t j", t=PACK)[:, m0:m1],
+            )
+
+        def interleave(engine, dst, src):
+            copy_on(
+                engine,
+                dst[:].rearrange("p (c i t) -> p c t i", i=4, t=PACK),
+                src[:].rearrange("p t (c i) -> p c t i", i=4),
+            )
+
+        def product(codes, scales, rhs, rhs_scale, n, per_bank):
+            banks = []
+            for u in range(PACK // per_bank):
+                bank = psum.tile([P, 512], F32, name="bank")
+                for v in range(per_bank):
+                    t = u * per_bank + v
+                    nc.tensor.matmul_mx(
+                        out=bank[:, v * n : (v + 1) * n],
+                        lhsT=codes[:, t * P : (t + 1) * P].bitcast(FP8X4),
+                        lhsT_scale=scales[:, t * P : (t + 1) * P],
+                        rhs=rhs.bitcast(FP8X4),
+                        rhs_scale=rhs_scale,
+                        start=True,
+                        stop=True,
+                    )
+                banks.append(bank)
+            return banks
+
+        starts = [sum(CHUNKS[:c]) for c in range(len(CHUNKS))]
+        last = len(CHUNKS) - 1
+
+        xs = sbuf("xs", [P, T], U8)
+        nc.vector.memset(xs[:].bitcast(I32), 0)
+        w3s = sbuf("w3s", [P, N], U8)
+        nc.vector.memset(w3s[:].bitcast(I32), 0)
+
+        l_offs = load_list("offs", offs)
+        w1_raw = sbuf("w1_raw", [P, PACK, H], F32)
+        nc.sync.dma_start(w1_raw[:], w1.rearrange("(p j) c -> p j c", j=PACK))
+        l2 = load_list("n2", n2)
+        l1 = load_list("n1", n1)
+        load_scale_rows(xs, x_scales)
+        xw = sbuf("xw", [P, T], U32)
+        nc.sync.dma_start(xw[:].bitcast(I32), words_view(x_words))
+        w2_raw = sbuf("w2_raw", [P, PACK, H], F32)
+        nc.sync.dma_start(w2_raw[:], w2.rearrange("(p j) c -> p j c", j=PACK))
+        l3 = load_list("n3", n3)
+        l4 = load_list("n4", n4)
+        w3w = sbuf("w3w", [P, N], I32)
+        nc.sync.dma_start(w3w[:], words_view(w3_words))
+        load_scale_rows(w3s, w3_scales)
+        res_rows = res.rearrange("(p t) j -> p t j", t=PACK)
+        res_sb = []
+        for c, n in enumerate(CHUNKS):
+            r = sbuf(f"res{c}", [P, PACK, n], F32)
+            nc.sync.dma_start(r[:], res_rows[:, :, starts[c] : starts[c] + n])
+            res_sb.append(r)
+
+        xs_picked = sbuf("xs_picked", [P, S], U8)
+        nc.vector.tensor_copy(xs_picked[:], xs[:].indirect(l_offs[:]))
+        w1_bf = sbuf("w1_bf", [P, PACK * H], BF16)
+        deal_weight("vector", w1_bf, w1_raw, 0, W1_ON_VECTOR)
+        deal_weight("scalar", w1_bf, w1_raw, W1_ON_VECTOR, P)
+        w1_codes = sbuf("w1_codes", [P, H], U32)
+        w1_scales = sbuf("w1_scales", [P, H], U8)
+        nc.vector.quantize_mx(out=w1_codes[:].bitcast(FP8X4), scales=w1_scales[:], in_=w1_bf[:])
+
+        half = S // 2
+        picked = []
+        for a in range(2):
+            xp = sbuf(f"xw_picked{a}", [P, half], U32)
+            nc.vector.tensor_copy(xp[:], xw[:].indirect(entries(l_offs, a * half, half)))
+            picked.append(xp)
+        y = [sbuf(f"y{t}", [P, S], F32) for t in range(PACK)]
+        for t in range(PACK):
+            for a in range(2):
+                bank = psum.tile([P, 512], F32, name="bank")
+                nc.tensor.matmul_mx(
+                    out=bank[:, :half],
+                    lhsT=w1_codes[:, t * P : (t + 1) * P].bitcast(FP8X4),
+                    lhsT_scale=w1_scales[:, t * P : (t + 1) * P],
+                    rhs=picked[a][:].bitcast(FP8X4),
+                    rhs_scale=xs_picked[:, a * half : (a + 1) * half],
+                    start=True,
+                    stop=True,
+                )
+                nc.scalar.copy(y[t][:, a * half : (a + 1) * half], bank[:, :half])
+
+        w2_bf = sbuf("w2_bf", [P, PACK * H], BF16)
+        deal_weight("scalar", w2_bf, w2_raw, 0, P)
+        w2_codes = sbuf("w2_codes", [P, H], U32)
+        w2_scales = sbuf("w2_scales", [P, H], U8)
+        nc.vector.quantize_mx(out=w2_codes[:].bitcast(FP8X4), scales=w2_scales[:], in_=w2_bf[:])
+
+        h = [sbuf(f"h{t}", [P, S], F32) for t in range(PACK)]
+        h_banks = []
+        steps = [(c, t) for c in range(len(CHUNKS)) for t in range(PACK)]
+        scaled = {}
+        zf = [sbuf(f"zf{c}", [P, PACK, n], F32) for c, n in enumerate(CHUNKS)]
+        w3_codes = None
+        for i in range(len(steps) + 1):
+            if i < len(steps):
+                c, t = steps[i]
+                tag = f"zb{c - 2}" if (c >= 2 and t == 0) else f"ring{i % RING}"
+                scaled[i] = sbuf(f"scaled{i}", [P, CHUNKS[c]], F32, tag)
+                nc.vector.tensor_scalar(scaled[i][:], y[t][:].indirect(entries(l2, starts[c], CHUNKS[c])), 0.75, 0.0, ALU.mult, ALU.add)
+            if i == 0:
+                continue
+            c, t = steps[i - 1]
+            n = CHUNKS[c]
+            nc.vector.tensor_tensor(zf[c][:, t, :], y[t][:].indirect(entries(l1, starts[c], n)), scaled[i - 1][:], ALU.add)
+            if t < PACK - 1:
+                continue
+            if c == last:
+                w3_codes = sbuf("w3_codes", [P, N], I32, f"ring{(i - 2) % RING}")
+                nc.vector.tensor_copy(w3_codes[:].rearrange("p (t m) -> p m t", t=PACK), w3w[:].rearrange("p (m t) -> p m t", t=PACK))
+            zb = sbuf(f"zb{c}", [P, PACK * n], BF16)
+            interleave("vector" if c == last else "scalar", zb, zf[c])
+            z_codes = sbuf(f"z_codes{c}", [P, n], U32)
+            z_scales = sbuf(f"z_scales{c}", [P, n], U8)
+            nc.vector.quantize_mx(out=z_codes[:].bitcast(FP8X4), scales=z_scales[:], in_=zb[:])
+            banks = product(w2_codes, w2_scales, z_codes[:], z_scales[:], n, 2)
+            for t in range(PACK):
+                nc.scalar.copy(h[t][:, starts[c] : starts[c] + n], banks[t // 2][:, (t % 2) * n : (t % 2 + 1) * n])
+            h_banks.append(banks)
+
+        w3_dealt = sbuf("w3_dealt", [P, N], U8, f"zb{last}")
+        nc.vector.tensor_copy(w3_dealt[:].rearrange("p (t m) -> p m t", t=PACK), w3s[:].rearrange("p (m t) -> p m t", t=PACK))
+
+        out_rows = out_0.rearrange("(p t) j -> p t j", t=PACK)
+        o_codes = sbuf("o_codes", [P, S], U32)
+        o_scales = sbuf("o_scales", [P, S], U8)
+        for c, n in enumerate(CHUNKS):
+            c0 = starts[c]
+            tail = "vector" if c == last else "scalar"
+            hb = sbuf(f"hb{c}", [P, PACK * n], BF16, f"ring{(len(steps) - 1) % RING}")
+            for u in range(2):
+                nc.scalar.copy(hb[:, 2 * u * n : 2 * (u + 1) * n], h_banks[c][u][:, : 2 * n])
+            g3 = sbuf(f"g3_{c}", [P, PACK * n], BF16, f"res{c - 2}" if c >= 2 else "g3")
+            g4 = sbuf(f"g4_{c}", [P, PACK * n], BF16, "g4")
+            larger = sbuf(f"larger{c}", [P, PACK * n], BF16)
+            for t in range(PACK):
+                nc.vector.tensor_copy(g3[:, t * n : (t + 1) * n], h[t][:].indirect(entries(l3, c0, n)))
+            for t in range(PACK):
+                if t == PACK - 1:
+                    nc.vector.tensor_tensor(larger[:], hb[:], g3[:], ALU.max)
+                nc.vector.tensor_copy(g4[:, t * n : (t + 1) * n], h[t][:].indirect(entries(l4, c0, n)))
+            z2 = sbuf(f"z2_{c}", [P, PACK, n], BF16)
+            nc.vector.tensor_tensor(z2[:].rearrange("p t n -> p (t n)"), larger[:], g4[:], ALU.min)
+            z2b = sbuf(f"z2b{c}", [P, PACK * n], BF16)
+            interleave(tail, z2b, z2)
+            z2_codes = sbuf(f"z2_codes{c}", [P, n], U32)
+            z2_scales = sbuf(f"z2_scales{c}", [P, n], U8)
+            nc.vector.quantize_mx(out=z2_codes[:].bitcast(FP8X4), scales=z2_scales[:], in_=z2b[:])
+            banks = product(w3_codes, w3_dealt, z2_codes[:], z2_scales[:], n, 2)
+            o = sbuf(f"o{c}", [P, PACK, n], F32)
+            for u in range(2):
+                nc.vector.tensor_tensor(
+                    o[:, 2 * u : 2 * u + 2, :].rearrange("p t n -> p (t n)"),
+                    banks[u][:, : 2 * n],
+                    res_sb[c][:, 2 * u : 2 * u + 2, :].rearrange("p t n -> p (t n)"),
+                    ALU.add,
+                )
+            nc.sync.dma_start(out_rows[:, :, c0 : c0 + n], o[:])
+            ob = sbuf(f"ob{c}", [P, PACK * n], BF16)
+            interleave(tail, ob, o)
+            nc.vector.quantize_mx(out=o_codes[:, c0 : c0 + n].bitcast(FP8X4), scales=o_scales[:, c0 : c0 + n], in_=ob[:])
+            nc.sync.dma_start(words_view(out_1)[:, c0 : c0 + n], o_codes[:, c0 : c0 + n].bitcast(I32))
+        for q in range(4):
+            queue = nc.sync if q % 2 else nc.scalar
+            queue.dma_start(out_2[0][4 * q : 4 * q + 4, :].bitcast(I32), o_scales[32 * q : 32 * q + 4, :].bitcast(I32))

@@ -16,9 +16,11 @@ ALU = mybir.AluOpType
 
 P = 128
 PACK = 4
-CHUNKS = (256, 128, 128)
+HALF = S // 2
+QUARTER = S // 4
+BLOCKS = ((0, HALF), (HALF, QUARTER), (HALF + QUARTER, QUARTER))
+WINDOW = 2 * S
 W1_ON_VECTOR = 80
-RING = 3
 
 
 def tile_picked_deepsumminmx_none_po_kernel(tc, x_words, x_scales, w1, w2, w3_words, w3_scales, res, offs, n1, n2, n3, n4, out_0, out_1, out_2):
@@ -62,9 +64,15 @@ def tile_picked_deepsumminmx_none_po_kernel(tc, x_words, x_scales, w1, w2, w3_wo
         def interleave(engine, dst, src):
             copy_on(
                 engine,
-                dst[:].rearrange("p (c i t) -> p c t i", i=4, t=PACK),
-                src[:].rearrange("p t (c i) -> p c t i", i=4),
+                dst.rearrange("p (c i t) -> p c t i", i=4, t=PACK),
+                src.rearrange("p t (c i) -> p c t i", i=4),
             )
+
+        def quantise(codes, scales, src, c0, n):
+            nc.vector.quantize_mx(out=codes[:, c0 : c0 + n].bitcast(FP8X4), scales=scales[:, c0 : c0 + n], in_=src[:, PACK * c0 : PACK * (c0 + n)])
+
+        def planes(flat):
+            return flat.rearrange("p (t n) -> p t n", t=PACK)
 
         def product(codes, scales, rhs, rhs_scale, n, per_bank):
             banks = []
@@ -83,9 +91,6 @@ def tile_picked_deepsumminmx_none_po_kernel(tc, x_words, x_scales, w1, w2, w3_wo
                     )
                 banks.append(bank)
             return banks
-
-        starts = [sum(CHUNKS[:c]) for c in range(len(CHUNKS))]
-        last = len(CHUNKS) - 1
 
         xs = sbuf("xs", [P, T], U8)
         nc.vector.memset(xs[:].bitcast(I32), 0)
@@ -109,10 +114,13 @@ def tile_picked_deepsumminmx_none_po_kernel(tc, x_words, x_scales, w1, w2, w3_wo
         load_scale_rows(w3s, w3_scales)
         res_rows = res.rearrange("(p t) j -> p t j", t=PACK)
         res_sb = []
-        for c, n in enumerate(CHUNKS):
-            r = sbuf(f"res{c}", [P, PACK, n], F32)
-            nc.sync.dma_start(r[:], res_rows[:, :, starts[c] : starts[c] + n])
+        for b, (c0, n) in enumerate(BLOCKS):
+            r = sbuf(f"res{b}", [P, PACK * n], F32)
+            nc.sync.dma_start(planes(r[:]), res_rows[:, :, c0 : c0 + n])
             res_sb.append(r)
+
+        y = [sbuf(f"y{t}", [P, WINDOW], F32) for t in range(PACK)]
+        h = [sbuf(f"h{t}", [P, WINDOW], F32) for t in range(PACK)]
 
         xs_picked = sbuf("xs_picked", [P, S], U8)
         nc.vector.tensor_copy(xs_picked[:], xs[:].indirect(l_offs[:]))
@@ -123,107 +131,140 @@ def tile_picked_deepsumminmx_none_po_kernel(tc, x_words, x_scales, w1, w2, w3_wo
         w1_scales = sbuf("w1_scales", [P, H], U8)
         nc.vector.quantize_mx(out=w1_codes[:].bitcast(FP8X4), scales=w1_scales[:], in_=w1_bf[:])
 
-        half = S // 2
         picked = []
         for a in range(2):
-            xp = sbuf(f"xw_picked{a}", [P, half], U32)
-            nc.vector.tensor_copy(xp[:], xw[:].indirect(entries(l_offs, a * half, half)))
+            xp = sbuf(f"xw_picked{a}", [P, HALF], U32)
+            nc.vector.tensor_copy(xp[:], xw[:].indirect(entries(l_offs, a * HALF, HALF)))
             picked.append(xp)
-        y = [sbuf(f"y{t}", [P, S], F32) for t in range(PACK)]
-        for t in range(PACK):
+        for window in y + h:
+            nc.vector.memset(window[:, S:].bitcast(I32), 0)
+        for u in range(2):
             for a in range(2):
-                bank = psum.tile([P, 512], F32, name="bank")
-                nc.tensor.matmul_mx(
-                    out=bank[:, :half],
-                    lhsT=w1_codes[:, t * P : (t + 1) * P].bitcast(FP8X4),
-                    lhsT_scale=w1_scales[:, t * P : (t + 1) * P],
-                    rhs=picked[a][:].bitcast(FP8X4),
-                    rhs_scale=xs_picked[:, a * half : (a + 1) * half],
-                    start=True,
-                    stop=True,
-                )
-                nc.scalar.copy(y[t][:, a * half : (a + 1) * half], bank[:, :half])
+                for t in (2 * u, 2 * u + 1):
+                    bank = psum.tile([P, 512], F32, name="bank")
+                    nc.tensor.matmul_mx(
+                        out=bank[:, :HALF],
+                        lhsT=w1_codes[:, t * P : (t + 1) * P].bitcast(FP8X4),
+                        lhsT_scale=w1_scales[:, t * P : (t + 1) * P],
+                        rhs=picked[a][:].bitcast(FP8X4),
+                        rhs_scale=xs_picked[:, a * HALF : (a + 1) * HALF],
+                        start=True,
+                        stop=True,
+                    )
+                    nc.scalar.copy(y[t][:, a * HALF : (a + 1) * HALF], bank[:, :HALF])
 
-        w2_bf = sbuf("w2_bf", [P, PACK * H], BF16)
+        shared_z = sbuf("shared_z", [P, PACK * H + PACK * HALF], BF16)
+        w2_bf = shared_z[:, : PACK * H]
+        zb_first = shared_z[:, PACK * H :]
+        zf = [planes(sbuf("zf_first", [P, PACK * HALF], F32)[:]), planes(shared_z[:, PACK * HALF :].bitcast(F32))]
         deal_weight("scalar", w2_bf, w2_raw, 0, P)
         w2_codes = sbuf("w2_codes", [P, H], U32)
         w2_scales = sbuf("w2_scales", [P, H], U8)
-        nc.vector.quantize_mx(out=w2_codes[:].bitcast(FP8X4), scales=w2_scales[:], in_=w2_bf[:])
+        z_codes = sbuf("z_codes", [P, S], U32)
+        z_scales = sbuf("z_scales", [P, S], U8)
+        scaled_last = sbuf("scaled_last", [P, S], F32)
+        scaled = [w1_raw[:, t, :] for t in range(PACK - 1)] + [scaled_last[:]]
 
-        h = [sbuf(f"h{t}", [P, S], F32) for t in range(PACK)]
-        h_banks = []
-        steps = [(c, t) for c in range(len(CHUNKS)) for t in range(PACK)]
-        scaled = {}
-        zf = [sbuf(f"zf{c}", [P, PACK, n], F32) for c, n in enumerate(CHUNKS)]
-        w3_codes = None
-        for i in range(len(steps) + 1):
-            if i < len(steps):
-                c, t = steps[i]
-                tag = f"zb{c - 2}" if (c >= 2 and t == 0) else f"ring{i % RING}"
-                scaled[i] = sbuf(f"scaled{i}", [P, CHUNKS[c]], F32, tag)
-                nc.vector.tensor_scalar(scaled[i][:], y[t][:].indirect(entries(l2, starts[c], CHUNKS[c])), 0.75, 0.0, ALU.mult, ALU.add)
-            if i == 0:
-                continue
-            c, t = steps[i - 1]
-            n = CHUNKS[c]
-            nc.vector.tensor_tensor(zf[c][:, t, :], y[t][:].indirect(entries(l1, starts[c], n)), scaled[i - 1][:], ALU.add)
-            if t < PACK - 1:
-                continue
-            if c == last:
-                w3_codes = sbuf("w3_codes", [P, N], I32, f"ring{(i - 2) % RING}")
-                nc.vector.tensor_copy(w3_codes[:].rearrange("p (t m) -> p m t", t=PACK), w3w[:].rearrange("p (m t) -> p m t", t=PACK))
-            zb = sbuf(f"zb{c}", [P, PACK * n], BF16)
-            interleave("vector" if c == last else "scalar", zb, zf[c])
-            z_codes = sbuf(f"z_codes{c}", [P, n], U32)
-            z_scales = sbuf(f"z_scales{c}", [P, n], U8)
-            nc.vector.quantize_mx(out=z_codes[:].bitcast(FP8X4), scales=z_scales[:], in_=zb[:])
-            banks = product(w2_codes, w2_scales, z_codes[:], z_scales[:], n, 2)
+        def sum_of_lookups(a, t):
+            nc.vector.tensor_tensor(zf[a][:, t, :], y[t][:].indirect(entries(l1, a * HALF, HALF)), scaled[t][:, a * HALF : (a + 1) * HALF], ALU.add)
+
+        def second_product(a, per_bank):
+            cols = slice(a * HALF, (a + 1) * HALF)
+            banks = product(w2_codes, w2_scales, z_codes[:, cols], z_scales[:, cols], HALF, per_bank)
             for t in range(PACK):
-                nc.scalar.copy(h[t][:, starts[c] : starts[c] + n], banks[t // 2][:, (t % 2) * n : (t % 2 + 1) * n])
-            h_banks.append(banks)
+                v = t % per_bank
+                nc.scalar.copy(h[t][:, cols], banks[t // per_bank][:, v * HALF : (v + 1) * HALF])
 
-        w3_dealt = sbuf("w3_dealt", [P, N], U8, f"zb{last}")
+        for t in range(PACK + 1):
+            if t < PACK:
+                nc.vector.tensor_scalar(scaled[t], y[t][:].indirect(l2[:]), 0.75, 0.0, ALU.mult, ALU.add)
+            if t > 0:
+                sum_of_lookups(0, t - 1)
+        interleave("scalar", zb_first, zf[0])
+        for a in (1, 0):
+            quantise(w2_codes, w2_scales, w2_bf, a * HALF, HALF)
+        for a in range(2):
+            quantise(z_codes, z_scales, zb_first, a * QUARTER, QUARTER)
+        second_product(0, 2)
+        for t in range(PACK):
+            sum_of_lookups(1, t)
+        w3_dealt = sbuf("w3_dealt", [P, N], U8, "w1_raw")
         nc.vector.tensor_copy(w3_dealt[:].rearrange("p (t m) -> p m t", t=PACK), w3s[:].rearrange("p (m t) -> p m t", t=PACK))
+        for a, engine in enumerate(("scalar", "vector")):
+            c0 = HALF + a * QUARTER
+            interleave(engine, w1_bf[:, PACK * c0 : PACK * (c0 + QUARTER)], zf[1][:, :, a * QUARTER : (a + 1) * QUARTER])
+        for a in range(2):
+            quantise(z_codes, z_scales, w1_bf, HALF + a * QUARTER, QUARTER)
+        second_product(1, 1)
+        w3_codes = sbuf("w3_codes", [P, N], I32, "w1_bf")
+        nc.vector.tensor_copy(w3_codes[:].rearrange("p (t m) -> p m t", t=PACK), w3w[:].rearrange("p (m t) -> p m t", t=PACK))
 
+        hb = sbuf("hb", [P, PACK, S], BF16)
+        for t in range(PACK):
+            nc.scalar.copy(hb[:, t, :], h[t][:, :S])
+        shared_z2 = sbuf("shared_z2", [P, PACK * S + PACK * HALF], BF16)
+        g3 = planes(shared_z2[:, : PACK * S])
+        late = PACK * S - 3 * HALF
+        g4 = [planes(sbuf("g4_first", [P, PACK * HALF], BF16)[:]), planes(shared_z2[:, late : late + PACK * HALF])]
+        z2b = [shared_z2[:, PACK * S :], sbuf("z2b1", [P, PACK * QUARTER], BF16)[:], sbuf("z2b2", [P, PACK * QUARTER], BF16)[:]]
+        larger = [planes(sbuf(f"larger{a}", [P, PACK * HALF], BF16)[:]) for a in range(2)]
+        z2 = [planes(sbuf(f"z2_{b}", [P, PACK * n], BF16)[:]) for b, (c0, n) in enumerate(BLOCKS)]
+        z2_codes = [sbuf(f"z2_codes{b}", [P, n], U32) for b, (c0, n) in enumerate(BLOCKS)]
+        z2_scales = [sbuf(f"z2_scales{b}", [P, n], U8) for b, (c0, n) in enumerate(BLOCKS)]
         out_rows = out_0.rearrange("(p t) j -> p t j", t=PACK)
         o_codes = sbuf("o_codes", [P, S], U32)
         o_scales = sbuf("o_scales", [P, S], U8)
-        for c, n in enumerate(CHUNKS):
-            c0 = starts[c]
-            tail = "vector" if c == last else "scalar"
-            hb = sbuf(f"hb{c}", [P, PACK * n], BF16, f"ring{(len(steps) - 1) % RING}")
-            for u in range(2):
-                nc.scalar.copy(hb[:, 2 * u * n : 2 * (u + 1) * n], h_banks[c][u][:, : 2 * n])
-            g3 = sbuf(f"g3_{c}", [P, PACK * n], BF16, f"res{c - 2}" if c >= 2 else "g3")
-            g4 = sbuf(f"g4_{c}", [P, PACK * n], BF16, "g4")
-            larger = sbuf(f"larger{c}", [P, PACK * n], BF16)
+        ob = sbuf("ob", [P, PACK * S], BF16)
+        engines = ("scalar", "scalar", "vector")
+
+        def fourth_lookups(a):
             for t in range(PACK):
-                nc.vector.tensor_copy(g3[:, t * n : (t + 1) * n], h[t][:].indirect(entries(l3, c0, n)))
-            for t in range(PACK):
-                if t == PACK - 1:
-                    nc.vector.tensor_tensor(larger[:], hb[:], g3[:], ALU.max)
-                nc.vector.tensor_copy(g4[:, t * n : (t + 1) * n], h[t][:].indirect(entries(l4, c0, n)))
-            z2 = sbuf(f"z2_{c}", [P, PACK, n], BF16)
-            nc.vector.tensor_tensor(z2[:].rearrange("p t n -> p (t n)"), larger[:], g4[:], ALU.min)
-            z2b = sbuf(f"z2b{c}", [P, PACK * n], BF16)
-            interleave(tail, z2b, z2)
-            z2_codes = sbuf(f"z2_codes{c}", [P, n], U32)
-            z2_scales = sbuf(f"z2_scales{c}", [P, n], U8)
-            nc.vector.quantize_mx(out=z2_codes[:].bitcast(FP8X4), scales=z2_scales[:], in_=z2b[:])
-            banks = product(w3_codes, w3_dealt, z2_codes[:], z2_scales[:], n, 2)
-            o = sbuf(f"o{c}", [P, PACK, n], F32)
-            for u in range(2):
-                nc.vector.tensor_tensor(
-                    o[:, 2 * u : 2 * u + 2, :].rearrange("p t n -> p (t n)"),
-                    banks[u][:, : 2 * n],
-                    res_sb[c][:, 2 * u : 2 * u + 2, :].rearrange("p t n -> p (t n)"),
-                    ALU.add,
-                )
-            nc.sync.dma_start(out_rows[:, :, c0 : c0 + n], o[:])
-            ob = sbuf(f"ob{c}", [P, PACK * n], BF16)
-            interleave(tail, ob, o)
-            nc.vector.quantize_mx(out=o_codes[:, c0 : c0 + n].bitcast(FP8X4), scales=o_scales[:, c0 : c0 + n], in_=ob[:])
+                nc.vector.tensor_copy(g4[a][:, t, :], h[t][:].indirect(entries(l4, a * HALF, HALF)))
+
+        def smaller(b):
+            c0, n = BLOCKS[b]
+            a, off = divmod(c0, HALF)
+            nc.vector.tensor_tensor(z2[b], larger[a][:, :, off : off + n], g4[a][:, :, off : off + n], ALU.min)
+
+        def third_product(b):
+            c0, n = BLOCKS[b]
+            for a in range(n // QUARTER):
+                quantise(z2_codes[b], z2_scales[b], z2b[b], a * QUARTER, QUARTER)
+            return product(w3_codes, w3_dealt, z2_codes[b][:], z2_scales[b][:], n, 512 // n)
+
+        def add_residual(b, banks):
+            c0, n = BLOCKS[b]
+            o = sbuf(f"o{b}", [P, PACK * n], F32)
+            for u, bank in enumerate(banks):
+                nc.vector.tensor_tensor(o[:, 512 * u : 512 * (u + 1)], bank[:], res_sb[b][:, 512 * u : 512 * (u + 1)], ALU.add)
+            nc.sync.dma_start(out_rows[:, :, c0 : c0 + n], planes(o[:]))
+            interleave(engines[b], ob[:, PACK * c0 : PACK * (c0 + n)], planes(o[:]))
+
+        def hand_on(b):
+            c0, n = BLOCKS[b]
+            quantise(o_codes, o_scales, ob, c0, n)
             nc.sync.dma_start(words_view(out_1)[:, c0 : c0 + n], o_codes[:, c0 : c0 + n].bitcast(I32))
+
+        for t in range(PACK):
+            nc.vector.tensor_copy(g3[:, t, :], h[t][:].indirect(l3[:]))
+        fourth_lookups(0)
+        for a in range(2):
+            cols = slice(a * HALF, (a + 1) * HALF)
+            nc.vector.tensor_tensor(larger[a], hb[:, :, cols], g3[:, :, cols], ALU.max)
+        smaller(0)
+        interleave(engines[0], z2b[0], z2[0])
+        banks = {0: third_product(0)}
+        fourth_lookups(1)
+        for b in (1, 2):
+            smaller(b)
+        for b in (1, 2):
+            interleave(engines[b], z2b[b], z2[b])
+        for b in (1, 2):
+            banks[b] = third_product(b)
+        for b in (0, 1, 2):
+            add_residual(b, banks[b])
+        for b in (0, 1, 2):
+            hand_on(b)
         for q in range(4):
             queue = nc.sync if q % 2 else nc.scalar
             queue.dma_start(out_2[0][4 * q : 4 * q + 4, :].bitcast(I32), o_scales[32 * q : 32 * q + 4, :].bitcast(I32))

@@ -105,13 +105,15 @@ def tile_picked_deepsumminmx_none_po_kernel(tc, x_words, x_scales, w1, w2, w3_wo
         load_scale_rows(xs, x_scales)
         xw = sbuf("xw", [P, T], U32)
         nc.sync.dma_start(xw[:].bitcast(I32), words_view(x_words))
-        w2_raw = sbuf("w2_raw", [P, PACK, H], F32)
-        nc.sync.dma_start(w2_raw[:], w2.rearrange("(p j) c -> p j c", j=PACK))
-        l3 = load_list("n3", n3)
-        l4 = load_list("n4", n4)
+        load_scale_rows(w3s, w3_scales)
         w3w = sbuf("w3w", [P, N], I32)
         nc.sync.dma_start(w3w[:], words_view(w3_words))
-        load_scale_rows(w3s, w3_scales)
+        shared_z = sbuf("shared_z", [P, 3 * PACK * H], BF16)
+        w2_words = shared_z[:, PACK * H :].bitcast(F32)
+        nc.sync.dma_start(w2_words, w2.rearrange("(p j) c -> p (j c)", j=PACK))
+        w2_raw = planes(w2_words)
+        l3 = load_list("n3", n3)
+        l4 = load_list("n4", n4)
         res_rows = res.rearrange("(p t) j -> p t j", t=PACK)
         res_sb = []
         for b, (c0, n) in enumerate(BLOCKS):
@@ -136,6 +138,10 @@ def tile_picked_deepsumminmx_none_po_kernel(tc, x_words, x_scales, w1, w2, w3_wo
             xp = sbuf(f"xw_picked{a}", [P, HALF], U32)
             nc.vector.tensor_copy(xp[:], xw[:].indirect(entries(l_offs, a * HALF, HALF)))
             picked.append(xp)
+        w3_dealt = sbuf("w3_dealt", [P, N], U8)
+        nc.vector.tensor_copy(w3_dealt[:].rearrange("p (t m) -> p m t", t=PACK), w3s[:].rearrange("p (m t) -> p m t", t=PACK))
+        w3_codes = sbuf("w3_codes", [P, N], I32)
+        nc.vector.tensor_copy(w3_codes[:].rearrange("p (t m) -> p m t", t=PACK), w3w[:].rearrange("p (m t) -> p m t", t=PACK))
         for window in y + h:
             nc.vector.memset(window[:, S:].bitcast(I32), 0)
         for u in range(2):
@@ -153,17 +159,15 @@ def tile_picked_deepsumminmx_none_po_kernel(tc, x_words, x_scales, w1, w2, w3_wo
                     )
                     nc.scalar.copy(y[t][:, a * HALF : (a + 1) * HALF], bank[:, :HALF])
 
-        shared_z = sbuf("shared_z", [P, PACK * H + PACK * HALF], BF16)
         w2_bf = shared_z[:, : PACK * H]
-        zb_first = shared_z[:, PACK * H :]
-        zf = [planes(sbuf("zf_first", [P, PACK * HALF], F32)[:]), planes(shared_z[:, PACK * HALF :].bitcast(F32))]
+        zb_first = shared_z[:, PACK * H : PACK * (H + HALF)]
+        zf = [planes(sbuf("zf_first", [P, PACK * HALF], F32)[:]), planes(shared_z[:, PACK * HALF : PACK * (H + HALF)].bitcast(F32))]
         deal_weight("scalar", w2_bf, w2_raw, 0, P)
         w2_codes = sbuf("w2_codes", [P, H], U32)
         w2_scales = sbuf("w2_scales", [P, H], U8)
         z_codes = sbuf("z_codes", [P, S], U32)
         z_scales = sbuf("z_scales", [P, S], U8)
-        scaled_last = sbuf("scaled_last", [P, S], F32)
-        scaled = [w1_raw[:, t, :] for t in range(PACK - 1)] + [scaled_last[:]]
+        scaled = [w1_raw[:, t, :] for t in range(PACK)]
 
         def sum_of_lookups(a, t):
             nc.vector.tensor_tensor(zf[a][:, t, :], y[t][:].indirect(entries(l1, a * HALF, HALF)), scaled[t][:, a * HALF : (a + 1) * HALF], ALU.add)
@@ -188,16 +192,25 @@ def tile_picked_deepsumminmx_none_po_kernel(tc, x_words, x_scales, w1, w2, w3_wo
         second_product(0, 2)
         for t in range(PACK):
             sum_of_lookups(1, t)
-        w3_dealt = sbuf("w3_dealt", [P, N], U8, "w1_raw")
-        nc.vector.tensor_copy(w3_dealt[:].rearrange("p (t m) -> p m t", t=PACK), w3s[:].rearrange("p (m t) -> p m t", t=PACK))
-        for a, engine in enumerate(("scalar", "vector")):
+        for a in range(2):
             c0 = HALF + a * QUARTER
-            interleave(engine, w1_bf[:, PACK * c0 : PACK * (c0 + QUARTER)], zf[1][:, :, a * QUARTER : (a + 1) * QUARTER])
+            interleave("vector", w1_bf[:, PACK * c0 : PACK * (c0 + QUARTER)], zf[1][:, :, a * QUARTER : (a + 1) * QUARTER])
         for a in range(2):
             quantise(z_codes, z_scales, w1_bf, HALF + a * QUARTER, QUARTER)
-        second_product(1, 1)
-        w3_codes = sbuf("w3_codes", [P, N], I32, "w1_bf")
-        nc.vector.tensor_copy(w3_codes[:].rearrange("p (t m) -> p m t", t=PACK), w3w[:].rearrange("p (m t) -> p m t", t=PACK))
+        for t in range(PACK):
+            for a in range(2):
+                cols = slice(HALF + a * QUARTER, HALF + (a + 1) * QUARTER)
+                bank = psum.tile([P, 512], F32, name="bank")
+                nc.tensor.matmul_mx(
+                    out=bank[:, :QUARTER],
+                    lhsT=w2_codes[:, t * P : (t + 1) * P].bitcast(FP8X4),
+                    lhsT_scale=w2_scales[:, t * P : (t + 1) * P],
+                    rhs=z_codes[:, cols].bitcast(FP8X4),
+                    rhs_scale=z_scales[:, cols],
+                    start=True,
+                    stop=True,
+                )
+                nc.scalar.copy(h[t][:, cols], bank[:, :QUARTER])
 
         hb = sbuf("hb", [P, PACK, S], BF16)
         for t in range(PACK):
@@ -237,7 +250,8 @@ def tile_picked_deepsumminmx_none_po_kernel(tc, x_words, x_scales, w1, w2, w3_wo
             o = sbuf(f"o{b}", [P, PACK * n], F32)
             for u, bank in enumerate(banks):
                 nc.vector.tensor_tensor(o[:, 512 * u : 512 * (u + 1)], bank[:], res_sb[b][:, 512 * u : 512 * (u + 1)], ALU.add)
-            nc.sync.dma_start(out_rows[:, :, c0 : c0 + n], planes(o[:]))
+                tiles = slice(u * 512 // n, (u + 1) * 512 // n)
+                nc.sync.dma_start(out_rows[:, tiles, c0 : c0 + n], planes(o[:])[:, tiles, :])
             interleave(engines[b], ob[:, PACK * c0 : PACK * (c0 + n)], planes(o[:]))
 
         def hand_on(b):

@@ -139,11 +139,13 @@ def tile_picked_deepsumminmx_none_po_kernel(tc, x_words, x_scales, w1, w2, w3_wo
             nc.vector.tensor_copy(xp[:], xw[:].indirect(entries(l_offs, a * HALF, HALF)))
             picked.append(xp)
         w3_dealt = sbuf("w3_dealt", [P, N], U8)
-        nc.vector.tensor_copy(w3_dealt[:].rearrange("p (t m) -> p m t", t=PACK), w3s[:].rearrange("p (m t) -> p m t", t=PACK))
+        nc.vector.tensor_copy(w3_dealt[:].rearrange("p (t m) -> p t m", t=PACK), w3s[:].rearrange("p (m t) -> p t m", t=PACK))
         w3_codes = sbuf("w3_codes", [P, N], I32)
         nc.vector.tensor_copy(w3_codes[:].rearrange("p (t m) -> p m t", t=PACK), w3w[:].rearrange("p (m t) -> p m t", t=PACK))
-        for window in y + h:
-            nc.vector.memset(window[:, S:].bitcast(I32), 0)
+        for window in y:
+            nc.vector.memset(window[:, S:], 0.0)
+        for window in h:
+            nc.scalar.copy(window[:, S:], y[0][:, S:])
         for u in range(2):
             for a in range(2):
                 for t in (2 * u, 2 * u + 1):
@@ -254,8 +256,8 @@ def tile_picked_deepsumminmx_none_po_kernel(tc, x_words, x_scales, w1, w2, w3_wo
                 nc.sync.dma_start(out_rows[:, tiles, c0 : c0 + n], planes(o[:])[:, tiles, :])
             interleave(engines[b], ob[:, PACK * c0 : PACK * (c0 + n)], planes(o[:]))
 
-        def hand_on(b):
-            c0, n = BLOCKS[b]
+        def hand_on(a):
+            c0, n = a * HALF, HALF
             quantise(o_codes, o_scales, ob, c0, n)
             nc.sync.dma_start(words_view(out_1)[:, c0 : c0 + n], o_codes[:, c0 : c0 + n].bitcast(I32))
 
@@ -277,8 +279,8 @@ def tile_picked_deepsumminmx_none_po_kernel(tc, x_words, x_scales, w1, w2, w3_wo
             banks[b] = third_product(b)
         for b in (0, 1, 2):
             add_residual(b, banks[b])
-        for b in (0, 1, 2):
-            hand_on(b)
+        for a in range(2):
+            hand_on(a)
         for q in range(4):
             queue = nc.sync if q % 2 else nc.scalar
             queue.dma_start(out_2[0][4 * q : 4 * q + 4, :].bitcast(I32), o_scales[32 * q : 32 * q + 4, :].bitcast(I32))

from contextlib import ExitStack

import concourse.mybir as mybir

K, T, S, N, H = 512, 2048, 512, 512, 512
FLOPS = 2 * K * H * S + 2 * H * H * S + 2 * H * N * S

F32 = mybir.dt.float32
BF16 = mybir.dt.bfloat16
U32 = mybir.dt.uint32
I32 = mybir.dt.int32
U16 = mybir.dt.uint16
U8 = mybir.dt.uint8
FP8X4 = mybir.dt.float8_e4m3fn_x4
ALU = mybir.AluOpType

P = 128
PACK = 4
HALF = S // 2
QUARTER = S // 4
BLOCKS = ((0, HALF), (HALF, QUARTER), (HALF + QUARTER, QUARTER))
WINDOW = 2 * S
W1_ON_VECTOR = 80


def tile_picked_deepsumminmx_none_po_kernel(tc, x_words, x_scales, w1, w2, w3_words, w3_scales, res, offs, n1, n2, n3, n4, out_0, out_1, out_2):
    nc = tc.nc
    with ExitStack() as ctx:
        lists = ctx.enter_context(tc.tile_pool(name="lists", bufs=1))
        sb = ctx.enter_context(tc.tile_pool(name="sb", bufs=1))
        psum = ctx.enter_context(tc.psum_pool(name="psum", bufs=8))

        def sbuf(name, shape, dtype, tag=None):
            return sb.tile(shape, dtype, name=name, tag=tag or name, align_bytes=64)

        def load_list(name, src):
            t = lists.tile([P, S // 16], U16, name=name)
            nc.sync.dma_start(t[:], src)
            return t

        def load_scale_rows(dst, src):
            for q in range(4):
                nc.sync.dma_start(dst[32 * q : 32 * q + 4, :].bitcast(I32), src[0][4 * q : 4 * q + 4, :].bitcast(I32))

        def words_view(dram):
            return dram[0].rearrange("p n t -> p (n t)").bitcast(I32)

        def entries(lst, c0, n):
            return lst[:, c0 // 16 : (c0 + n) // 16]

        def copy_on(engine, out, in_):
            if engine == "vector":
                nc.vector.tensor_copy(out, in_)
            else:
                nc.scalar.copy(out, in_)

        def deal_weight(engine, dst, raw, m0, m1):
            copy_on(
                engine,
                dst[:].rearrange("p (t m j) -> p m t j", t=PACK, j=PACK)[:, m0:m1],
                raw[:].rearrange("p j (m t) -> p m t j", t=PACK)[:, m0:m1],
            )

        def interleave(engine, dst, src):
            copy_on(
                engine,
                dst.rearrange("p (c i t) -> p c t i", i=4, t=PACK),
                src.rearrange("p t (c i) -> p c t i", i=4),
            )

        def quantise(codes, scales, src, c0, n):
            nc.vector.quantize_mx(out=codes[:, c0 : c0 + n].bitcast(FP8X4), scales=scales[:, c0 : c0 + n], in_=src[:, PACK * c0 : PACK * (c0 + n)])

        def planes(flat):
            return flat.rearrange("p (t n) -> p t n", t=PACK)

        def product(codes, scales, rhs, rhs_scale, n, per_bank):
            banks = []
            for u in range(PACK // per_bank):
                bank = psum.tile([P, 512], F32, name="bank")
                for v in range(per_bank):
                    t = u * per_bank + v
                    nc.tensor.matmul_mx(
                        out=bank[:, v * n : (v + 1) * n],
                        lhsT=codes[:, t * P : (t + 1) * P].bitcast(FP8X4),
                        lhsT_scale=scales[:, t * P : (t + 1) * P],
                        rhs=rhs.bitcast(FP8X4),
                        rhs_scale=rhs_scale,
                        start=True,
                        stop=True,
                    )
                banks.append(bank)
            return banks

        xs = sbuf("xs", [P, T], U8)
        nc.vector.memset(xs[:].bitcast(I32), 0)
        w3s = sbuf("w3s", [P, N], U8)
        nc.vector.memset(w3s[:].bitcast(I32), 0)

        l_offs = load_list("offs", offs)
        w1_raw = sbuf("w1_raw", [P, PACK, H], F32)
        nc.sync.dma_start(w1_raw[:], w1.rearrange("(p j) c -> p j c", j=PACK))
        l2 = load_list("n2", n2)
        l1 = load_list("n1", n1)
        load_scale_rows(xs, x_scales)
        xw = sbuf("xw", [P, T], U32)
        nc.sync.dma_start(xw[:].bitcast(I32), words_view(x_words))
        load_scale_rows(w3s, w3_scales)
        w3w = sbuf("w3w", [P, N], I32)
        nc.sync.dma_start(w3w[:], words_view(w3_words))
        shared_z = sbuf("shared_z", [P, 3 * PACK * H], BF16)
        w2_words = shared_z[:, PACK * H :].bitcast(F32)
        nc.sync.dma_start(w2_words, w2.rearrange("(p j) c -> p (j c)", j=PACK))
        w2_raw = planes(w2_words)
        l3 = load_list("n3", n3)
        l4 = load_list("n4", n4)
        res_rows = res.rearrange("(p t) j -> p t j", t=PACK)
        res_sb = []
        for b, (c0, n) in enumerate(BLOCKS):
            r = sbuf(f"res{b}", [P, PACK * n], F32)
            nc.sync.dma_start(planes(r[:]), res_rows[:, :, c0 : c0 + n])
            res_sb.append(r)

        y = [sbuf(f"y{t}", [P, WINDOW], F32) for t in range(PACK)]
        h = [sbuf(f"h{t}", [P, WINDOW], F32) for t in range(PACK)]

        xs_picked = sbuf("xs_picked", [P, S], U8)
        nc.vector.tensor_copy(xs_picked[:], xs[:].indirect(l_offs[:]))
        w1_bf = sbuf("w1_bf", [P, PACK * H], BF16)
        deal_weight("vector", w1_bf, w1_raw, 0, W1_ON_VECTOR)
        deal_weight("scalar", w1_bf, w1_raw, W1_ON_VECTOR, P)
        w1_codes = sbuf("w1_codes", [P, H], U32)
        w1_scales = sbuf("w1_scales", [P, H], U8)
        nc.vector.quantize_mx(out=w1_codes[:].bitcast(FP8X4), scales=w1_scales[:], in_=w1_bf[:])

        picked = []
        for a in range(2):
            xp = sbuf(f"xw_picked{a}", [P, HALF], U32)
            nc.vector.tensor_copy(xp[:], xw[:].indirect(entries(l_offs, a * HALF, HALF)))
            picked.append(xp)
        w3_dealt = sbuf("w3_dealt", [P, N], U8)
        nc.vector.tensor_copy(w3_dealt[:].rearrange("p (t m) -> p t m", t=PACK), w3s[:].rearrange("p (m t) -> p t m", t=PACK))
        w3_codes = sbuf("w3_codes", [P, N], I32)
        nc.vector.tensor_copy(w3_codes[:].rearrange("p (t m) -> p m t", t=PACK), w3w[:].rearrange("p (m t) -> p m t", t=PACK))
        for window in y:
            nc.vector.memset(window[:, S:], 0.0)
        for window in h:
            nc.scalar.copy(window[:, S:], y[0][:, S:])
        for u in range(2):
            for a in range(2):
                for t in (2 * u, 2 * u + 1):
                    bank = psum.tile([P, 512], F32, name="bank")
                    nc.tensor.matmul_mx(
                        out=bank[:, :HALF],
                        lhsT=w1_codes[:, t * P : (t + 1) * P].bitcast(FP8X4),
                        lhsT_scale=w1_scales[:, t * P : (t + 1) * P],
                        rhs=picked[a][:].bitcast(FP8X4),
                        rhs_scale=xs_picked[:, a * HALF : (a + 1) * HALF],
                        start=True,
                        stop=True,
                    )
                    nc.scalar.copy(y[t][:, a * HALF : (a + 1) * HALF], bank[:, :HALF])

        w2_bf = shared_z[:, : PACK * H]
        zb_first = shared_z[:, PACK * H : PACK * (H + HALF)]
        zf = [planes(sbuf("zf_first", [P, PACK * HALF], F32)[:]), planes(shared_z[:, PACK * HALF : PACK * (H + HALF)].bitcast(F32))]
        deal_weight("scalar", w2_bf, w2_raw, 0, P)
        w2_codes = sbuf("w2_codes", [P, H], U32)
        w2_scales = sbuf("w2_scales", [P, H], U8)
        z_codes = sbuf("z_codes", [P, S], U32)
        z_scales = sbuf("z_scales", [P, S], U8)
        scaled = [w1_raw[:, t, :] for t in range(PACK)]

        def sum_of_lookups(a, t):
            nc.vector.tensor_tensor(zf[a][:, t, :], y[t][:].indirect(entries(l1, a * HALF, HALF)), scaled[t][:, a * HALF : (a + 1) * HALF], ALU.add)

        def second_product(a, per_bank):
            cols = slice(a * HALF, (a + 1) * HALF)
            banks = product(w2_codes, w2_scales, z_codes[:, cols], z_scales[:, cols], HALF, per_bank)
            for t in range(PACK):
                v = t % per_bank
                nc.scalar.copy(h[t][:, cols], banks[t // per_bank][:, v * HALF : (v + 1) * HALF])

        for t in range(PACK + 1):
            if t < PACK:
                nc.vector.tensor_scalar(scaled[t], y[t][:].indirect(l2[:]), 0.75, 0.0, ALU.mult, ALU.add)
            if t > 0:
                sum_of_lookups(0, t - 1)
        interleave("scalar", zb_first, zf[0])
        for a in (1, 0):
            quantise(w2_codes, w2_scales, w2_bf, a * HALF, HALF)
        for a in range(2):
            quantise(z_codes, z_scales, zb_first, a * QUARTER, QUARTER)
        second_product(0, 2)
        for t in range(PACK):
            sum_of_lookups(1, t)
        for a in range(2):
            c0 = HALF + a * QUARTER
            interleave("vector", w1_bf[:, PACK * c0 : PACK * (c0 + QUARTER)], zf[1][:, :, a * QUARTER : (a + 1) * QUARTER])
        for a in range(2):
            quantise(z_codes, z_scales, w1_bf, HALF + a * QUARTER, QUARTER)
        for t in range(PACK):
            for a in range(2):
                cols = slice(HALF + a * QUARTER, HALF + (a + 1) * QUARTER)
                bank = psum.tile([P, 512], F32, name="bank")
                nc.tensor.matmul_mx(
                    out=bank[:, :QUARTER],
                    lhsT=w2_codes[:, t * P : (t + 1) * P].bitcast(FP8X4),
                    lhsT_scale=w2_scales[:, t * P : (t + 1) * P],
                    rhs=z_codes[:, cols].bitcast(FP8X4),
                    rhs_scale=z_scales[:, cols],
                    start=True,
                    stop=True,
                )
                nc.scalar.copy(h[t][:, cols], bank[:, :QUARTER])

        hb = sbuf("hb", [P, PACK, S], BF16)
        for t in range(PACK):
            nc.scalar.copy(hb[:, t, :], h[t][:, :S])
        shared_z2 = sbuf("shared_z2", [P, PACK * S + PACK * HALF], BF16)
        g3 = planes(shared_z2[:, : PACK * S])
        late = PACK * S - 3 * HALF
        g4 = [planes(sbuf("g4_first", [P, PACK * HALF], BF16)[:]), planes(shared_z2[:, late : late + PACK * HALF])]
        z2b = [shared_z2[:, PACK * S :], sbuf("z2b1", [P, PACK * QUARTER], BF16)[:], sbuf("z2b2", [P, PACK * QUARTER], BF16)[:]]
        larger = [planes(sbuf(f"larger{a}", [P, PACK * HALF], BF16)[:]) for a in range(2)]
        z2 = [planes(sbuf(f"z2_{b}", [P, PACK * n], BF16)[:]) for b, (c0, n) in enumerate(BLOCKS)]
        z2_codes = [sbuf(f"z2_codes{b}", [P, n], U32) for b, (c0, n) in enumerate(BLOCKS)]
        z2_scales = [sbuf(f"z2_scales{b}", [P, n], U8) for b, (c0, n) in enumerate(BLOCKS)]
        out_rows = out_0.rearrange("(p t) j -> p t j", t=PACK)
        o_codes = sbuf("o_codes", [P, S], U32)
        o_scales = sbuf("o_scales", [P, S], U8)
        ob = sbuf("ob", [P, PACK * S], BF16)
        engines = ("scalar", "scalar", "vector")

        def fourth_lookups(a):
            for t in range(PACK):
                nc.vector.tensor_copy(g4[a][:, t, :], h[t][:].indirect(entries(l4, a * HALF, HALF)))

        def smaller(b):
            c0, n = BLOCKS[b]
            a, off = divmod(c0, HALF)
            nc.vector.tensor_tensor(z2[b], larger[a][:, :, off : off + n], g4[a][:, :, off : off + n], ALU.min)

        def third_product(b):
            c0, n = BLOCKS[b]
            for a in range(n // QUARTER):
                quantise(z2_codes[b], z2_scales[b], z2b[b], a * QUARTER, QUARTER)
            return product(w3_codes, w3_dealt, z2_codes[b][:], z2_scales[b][:], n, 512 // n)

        def add_residual(b, banks):
            c0, n = BLOCKS[b]
            o = sbuf(f"o{b}", [P, PACK * n], F32)
            for u, bank in enumerate(banks):
                nc.vector.tensor_tensor(o[:, 512 * u : 512 * (u + 1)], bank[:], res_sb[b][:, 512 * u : 512 * (u + 1)], ALU.add)
                tiles = slice(u * 512 // n, (u + 1) * 512 // n)
                nc.sync.dma_start(out_rows[:, tiles, c0 : c0 + n], planes(o[:])[:, tiles, :])
            interleave(engines[b], ob[:, PACK * c0 : PACK * (c0 + n)], planes(o[:]))

        def hand_on(a):
            c0, n = a * HALF, HALF
            quantise(o_codes, o_scales, ob, c0, n)
            nc.sync.dma_start(words_view(out_1)[:, c0 : c0 + n], o_codes[:, c0 : c0 + n].bitcast(I32))

        for t in range(PACK):
            nc.vector.tensor_copy(g3[:, t, :], h[t][:].indirect(l3[:]))
        fourth_lookups(0)
        for a in range(2):
            cols = slice(a * HALF, (a + 1) * HALF)
            nc.vector.tensor_tensor(larger[a], hb[:, :, cols], g3[:, :, cols], ALU.max)
        smaller(0)
        interleave(engines[0], z2b[0], z2[0])
        banks = {0: third_product(0)}
        fourth_lookups(1)
        for b in (1, 2):
            smaller(b)
        for b in (1, 2):
            interleave(engines[b], z2b[b], z2[b])
        for b in (1, 2):
            banks[b] = third_product(b)
        for b in (0, 1, 2):
            add_residual(b, banks[b])
        for a in range(2):
            hand_on(a)
        for q in range(4):
            queue = nc.sync if q % 2 else nc.scalar
            queue.dma_start(out_2[0][4 * q : 4 * q + 4, :].bitcast(I32), o_scales[32 * q : 32 * q + 4, :].bitcast(I32))
